import numpy as np
import ml_dtypes


def mxq(x, axis, fmt="e4m3"):
    dtype, down = {"e4m3": (ml_dtypes.float8_e4m3fn, 7), "e5m2": (ml_dtypes.float8_e5m2, 14)}[fmt]
    v = np.moveaxis(np.asarray(x, np.float32).astype(ml_dtypes.bfloat16).astype(np.float64), axis, -1)
    blocks = v.reshape(v.shape[:-1] + (-1, 32))
    amax = np.abs(blocks).max(-1, keepdims=True)
    byte = np.maximum(np.where(amax > 0, np.frexp(amax)[1] - 1 + 127, 0) - down, 1)
    scale = np.exp2(byte - 127.0)
    codes = (blocks / scale).astype(np.float32).astype(dtype).astype(np.float64)
    return np.moveaxis((codes * scale).reshape(v.shape), -1, axis)


WIDE = False


def mx_kscale(k):
    if not WIDE:
        return np.ones(k)
    levels = np.array([10, -10, 5, -5, 0])
    if k % 512:
        return np.exp2(np.random.permutation(np.resize(levels, k // 32))).repeat(32)
    a = np.empty((k // 512, 16))
    for p in range(k // 512):
        a[p, :8] = np.random.permutation(np.resize(levels, 8))
        for g in range(8):
            far = levels[np.abs(levels - a[p, g]) >= 10]
            a[p, g + 8] = far[np.random.randint(len(far))]
    return np.exp2(a.ravel()).repeat(32)


def f64(x):
    return np.asarray(x).astype(np.float64)


def striped(idx):
    return np.tile(np.asarray(idx).reshape(-1, 16).T, (8, 1)).astype(np.uint16)


def unstriped(offs):
    return offs[:16].T.reshape(-1).astype(np.int64)


E2M1 = np.array([0.0, 0.5, 1.0, 1.5, 2.0, 3.0, 4.0, 6.0, -0.0, -0.5, -1.0, -1.5, -2.0, -3.0, -4.0, -6.0])


def pack_weight(w, fmt):
    k, n = w.shape
    w = f64(np.asarray(w, np.float32).astype(ml_dtypes.bfloat16)).reshape(k // 32, 32, n)
    amax = np.abs(w).max(1)
    if fmt == "e4m3":
        byte = np.frexp(amax)[1] - 1 + 127 - 7
    else:
        mant, ex = np.frexp(amax / 6.0)
        byte = np.where(mant > 0.5, ex, ex - 1) + 127
    byte = np.clip(np.where(amax > 0, byte, 1), 1, 254)
    scaled = (w * np.exp2(127.0 - byte)[:, None, :]).reshape(k, n).astype(np.float32)
    by_word = np.ascontiguousarray(scaled.reshape(k // 512, 128, 4, n).transpose(0, 1, 3, 2))
    if fmt == "e4m3":
        words = by_word.astype(ml_dtypes.float8_e4m3fn).view(np.uint8)
    else:
        c = by_word.astype(ml_dtypes.float4_e2m1fn).view(np.uint8) & 0xF
        words = (c[..., 0::2] | (c[..., 1::2] << 4)).reshape(k // 512, 128, 2 * n)
    return np.ascontiguousarray(words), np.ascontiguousarray(byte.astype(np.uint8).reshape(k // 512, 16, n))


def unpack_weight(words, scales, fmt):
    g, _, n = scales.shape
    words = np.ascontiguousarray(words).reshape(g, 128, n, -1)
    if fmt == "e4m3":
        vals = words.view(ml_dtypes.float8_e4m3fn).astype(np.float64)
    else:
        nib = np.empty((g, 128, n, 4), np.uint8)
        nib[..., 0::2] = words & 0xF
        nib[..., 1::2] = words >> 4
        vals = E2M1[nib]
    vals = vals * np.repeat(np.exp2(scales.astype(np.float64) - 127.0), 8, axis=1)[..., None]
    return vals.transpose(0, 1, 3, 2).reshape(g * 512, n)


def softplus(v):
    return np.log(1.0 + np.exp(v))


def sigmoid(v):
    return 1.0 / (1.0 + np.exp(-v))


D, E, T, I, Q, G = 512, 512, 2048, 512, 128, 64


def setup_inputs():
    n = np.random.standard_normal
    idx = np.random.permutation(T)[:I]
    fd = mx_kscale(D)
    fe = mx_kscale(E)
    keysp = pack_weight(n((D, T)) / fd[:, None], "e2m1")
    valsp = pack_weight(n((E, T)) / fe[:, None], "e2m1")
    return {
        "query": (n((D, Q)) * 0.8 / np.sqrt(D) * fd[:, None]).astype(np.float32),
        "query2": (n((D, Q)) * 1.0 / np.sqrt(D) * fd[:, None]).astype(np.float32),
        "keys_words": keysp[0],
        "keys_scales": keysp[1],
        "reserve": (np.random.uniform(2.0, 10.0, (Q, 1))).astype(np.float32),
        "gout": (n((E, Q)) * 1 / np.sqrt(E) * fe[:, None]).astype(np.float32),
        "vals_words": valsp[0],
        "vals_scales": valsp[1],
        "dquery2": (n((D, Q)) * 1.0 / np.sqrt(D) * fd[:, None]).astype(np.float32),
        "base": (0.5 * n((Q, T))).astype(np.float32),
        "offs": striped(idx),
    }


def reference(query, query2, keys_words, keys_scales, reserve, gout, vals_words, vals_scales, dquery2, base, offs):
    idx = unstriped(offs)
    keysu = unpack_weight(keys_words, keys_scales, "e2m1")
    valsu = unpack_weight(vals_words, vals_scales, "e2m1")
    queryq = mxq(f64(query), 0, "e4m3")
    keysidxg = keysu[:, idx]
    a = queryq.T @ keysidxg
    query2q = mxq(f64(query2), 0, "e4m3")
    b = query2q.T @ keysidxg
    dquery2q = mxq(f64(dquery2), 0, "e4m3")
    tb = dquery2q.T @ keysidxg
    m1 = b.reshape(Q, G, I // G).mean(axis=2)
    q0 = softplus(m1 * 3.0)
    z = np.sum(q0, axis=1, keepdims=True) + f64(reserve)
    pa = np.exp(a)
    s = pa.reshape(Q, G, I // G).sum(axis=2)
    goutq = mxq(f64(gout), 0, "e4m3")
    valsidxg = valsu[:, idx]
    c0 = goutq.T @ valsidxg
    drr = c0 * pa
    dr = drr.reshape(Q, G, I // G).sum(axis=2)
    dz = np.sum(dr * q0 / s / np.square(z) * (-1.0), axis=1, keepdims=True)
    dq0 = dr / z / s + dz
    tm1 = tb.reshape(Q, G, I // G).mean(axis=2)
    tq0 = tm1 * 3.0 * sigmoid(m1 * 3.0)
    tz = np.sum(tq0, axis=1, keepdims=True)
    tdz = np.sum((tq0 / s * dr - tz * z * 2.0 * dr * q0 / s / np.square(z)) / np.square(z) * (-1.0), axis=1, keepdims=True)
    tdq0 = tz * dr / np.square(z) * (-1.0) / s + tdz
    tdm1 = (tdq0 * sigmoid(m1 * 3.0) + tm1 * 3.0 * sigmoid(m1 * 3.0) * (1.0 - sigmoid(m1 * 3.0)) * dq0) * 3.0
    te1 = tdm1 / 8.0
    tr1 = np.repeat(te1, I // G, axis=1)
    gs = tr1 * 1024.0
    gf = np.zeros((Q, T))
    gf[:, idx] = gs
    y = f64(base) + gf
    return y

@@ -1,0 +1,211 @@
+from contextlib import ExitStack
+
+import concourse.mybir as mybir
+
+F32 = mybir.dt.float32
+BF16 = mybir.dt.bfloat16
+I32 = mybir.dt.int32
+U32 = mybir.dt.uint32
+U16 = mybir.dt.uint16
+U8 = mybir.dt.uint8
+FP8X4 = mybir.dt.float8_e4m3fn_x4
+FP4X4 = mybir.dt.float4_e2m1fn_x4
+ALU = mybir.AluOpType
+ACT = mybir.ActivationFunctionType
+AXIS_X = mybir.AxisListType.X
+
+P = 128
+PACK = 4
+POOL = 2048
+SLOTS = 512
+ROWS = 128
+PAGE = 8
+PAGES = SLOTS // PAGE
+STORE_WIDTHS = (256, 512, 512, 512, 256)
+
+FLOPS = 4 * 2 * 512 * ROWS * SLOTS
+
+
+def tile_attend_hvpagequotas_s_kernel(
+    tc, query, query2, keys_words, keys_scales, reserve, gout, vals_words, vals_scales, dquery2, base, offs, out
+):
+    nc = tc.nc
+    with ExitStack() as ctx:
+        sb = ctx.enter_context(tc.tile_pool(name="sb", bufs=1))
+        ps = ctx.enter_context(tc.psum_pool(name="ps", bufs=1))
+
+        def by_page(ap):
+            return ap.rearrange("p (g j) -> p g j", j=PAGE)
+
+        def over_page(ap):
+            return ap.unsqueeze(2).to_broadcast([P, PAGES, PAGE])
+
+        offsets = sb.tile([P, SLOTS // 16], U16, name="offsets")
+        key_bytes = sb.tile([P, POOL], U8, name="key_bytes", align_bytes=64)
+        val_bytes = sb.tile([P, POOL], U8, name="val_bytes", align_bytes=64)
+        key_words = sb.tile([P, POOL], U16, name="key_words", align_bytes=64)
+        val_words = sb.tile([P, POOL], U16, name="val_words", align_bytes=64)
+        half = sb.tile([P, 1], F32, name="half")
+        minus_one = sb.tile([P, 1], F32, name="minus_one")
+        abs_tanh = sb.tile([P, PAGES + 1], F32, name="abs_tanh")
+        relu_res = sb.tile([P, PAGES + 1], F32, name="relu_res")
+        placed = sb.tile([P, POOL], F32, name="placed")
+        base_sb = sb.tile([P, POOL], F32, name="base_sb")
+
+        def load_bytes(queue, tile, scales):
+            for quad in range(4):
+                queue.dma_start(
+                    out=tile[32 * quad : 32 * quad + 4, :].bitcast(I32),
+                    in_=scales[0, 4 * quad : 4 * quad + 4, :].bitcast(I32),
+                )
+
+        nc.vector.memset(key_bytes[:].bitcast(I32), 0)
+        nc.vector.memset(half[:], 0.5)
+        load_bytes(nc.scalar, key_bytes, keys_scales)
+        nc.scalar.activation(minus_one[:], half[:], ACT.Copy, scale=-2.0)
+        nc.vector.memset(val_bytes[:].bitcast(I32), 0)
+        nc.vector.memset(abs_tanh[:, PAGES : PAGES + 1], 1.0)
+        nc.vector.memset(placed[:], 0.0)
+
+        def load_rows(name, rows):
+            raw = sb.tile([P, PACK, ROWS], F32, name=name, tag=name)
+            nc.sync.dma_start(out=raw[:], in_=rows.rearrange("(p j) w -> p j w", j=PACK))
+            return raw
+
+        nc.sync.dma_start(offsets[:], offs)
+        nc.sync.dma_start(out=key_words[:].bitcast(I32), in_=keys_words[0].bitcast(I32))
+        raw_q2 = load_rows("raw_q2", query2)
+        raw_q = load_rows("raw_q", query)
+        load_bytes(nc.sync, val_bytes, vals_scales)
+        nc.sync.dma_start(out=val_words[:].bitcast(I32), in_=vals_words[0].bitcast(I32))
+        raw_dq2 = load_rows("raw_dq2", dquery2)
+        raw_gout = load_rows("raw_gout", gout)
+        nc.sync.dma_start(out=relu_res[:, PAGES : PAGES + 1], in_=reserve)
+        nc.sync.dma_start(out=base_sb[:], in_=base)
+
+        def gather(name, window, dtype, tag):
+            picked = sb.tile([P, SLOTS], dtype, name=name, tag=tag, align_bytes=64)
+            nc.vector.tensor_copy(picked[:], window[:].indirect(offsets[:]))
+            return picked
+
+        def interleave(name, raws):
+            woven = sb.tile([P, len(raws), ROWS, PACK], BF16, name=name, tag=name, align_bytes=64)
+            for n, raw in enumerate(raws):
+                nc.scalar.copy(out=woven[:, n], in_=raw[:].rearrange("p j w -> p w j"))
+            return woven
+
+        def quantise(name, woven, count):
+            codes = sb.tile([P, count * ROWS], U32, name=name + "_codes", align_bytes=64)
+            scales = sb.tile([P, count * ROWS], U8, name=name + "_scales", align_bytes=64)
+            nc.vector.quantize_mx(
+                out=codes[:].bitcast(FP8X4), scales=scales[:], in_=woven[:].rearrange("p n w j -> p (n w j)")
+            )
+            return codes, scales
+
+        def scores(name, rows, n, words, byts):
+            codes, scales = rows
+            bank = ps.tile([ROWS, SLOTS], F32, name=name)
+            cols = slice(n * ROWS, (n + 1) * ROWS)
+            nc.tensor.matmul_mx(
+                out=bank[:],
+                lhsT=codes[:, cols].bitcast(FP8X4),
+                lhsT_scale=scales[:, cols],
+                rhs=words[:].bitcast(FP4X4),
+                rhs_scale=byts[:],
+                start=True,
+                stop=True,
+            )
+            return bank
+
+        def small(name, width=PAGES):
+            return sb.tile([P, width], F32, name=name)
+
+        woven_a = interleave("woven_a", [raw_q2, raw_q])
+        woven_b = interleave("woven_b", [raw_dq2, raw_gout])
+
+        kb = gather("kb", key_bytes, U8, "kb")
+        kw = gather("kw", key_words, U16, "kw")
+        first = quantise("first", woven_a, 2)
+        b = scores("b", first, 0, kw, kb)
+        a = scores("a", first, 1, kw, kb)
+        vb = gather("vb", val_bytes, U8, "vb")
+
+        sum_b = small("sum_b")
+        nc.vector.tensor_reduce(sum_b[:], by_page(b[:]), AXIS_X, ALU.add)
+        top = small("top")
+        nc.vector.tensor_reduce(top[:], by_page(a[:]), AXIS_X, ALU.max)
+        shifted = small("shifted", SLOTS)
+        nc.vector.tensor_tensor(by_page(shifted[:]), by_page(a[:]), over_page(top[:]), ALU.subtract)
+
+        tanh = sb.tile([P, PAGES], F32, name="tanh", tag="raw_gout")
+        nc.scalar.activation(tanh[:], sum_b[:], ACT.Tanh, scale=3.0 / 16.0)
+        nc.scalar.activation(relu_res[:, :PAGES], sum_b[:], ACT.Relu, scale=3.0 / 8.0)
+        nc.scalar.activation(abs_tanh[:, :PAGES], tanh[:], ACT.Abs)
+        neg_t1 = small("neg_t1")
+        nc.scalar.activation(neg_t1[:], tanh[:], ACT.Identity, bias=minus_one[:], scale=-1.0)
+        pa = sb.tile([P, SLOTS], F32, name="pa", tag="raw_dq2")
+        nc.scalar.activation(pa[:], shifted[:], ACT.Exp)
+        log_sig = shifted[:, : PAGES + 1]
+        nc.scalar.activation(log_sig, abs_tanh[:], ACT.Ln, bias=half[:], scale=0.5)
+
+        second = quantise("second", woven_b, 2)
+        tb = scores("tb", second, 0, kw, kb)
+        vw = gather("vw", val_words, U16, "woven_b")
+        c0 = scores("c0", second, 1, vw, vb)
+
+        s = small("s")
+        nc.vector.tensor_reduce(s[:], by_page(pa[:]), AXIS_X, ALU.add)
+        inv_s = small("inv_s")
+        sum_tb = small("sum_tb")
+        nc.vector.tensor_reduce(sum_tb[:], by_page(tb[:]), AXIS_X, ALU.add)
+        nc.vector.reciprocal(inv_s[:], s[:])
+        drr = small("drr", SLOTS)
+        nc.vector.tensor_tensor(drr[:], c0[:], pa[:], ALU.mult)
+
+        neg_q0 = small("neg_q0", PAGES + 1)
+        neg_z = small("neg_z", 1)
+        nc.vector.scalar_tensor_tensor(
+            neg_q0[:], relu_res[:], -1.0, log_sig, ALU.mult, ALU.add, accum_out=neg_z[:]
+        )
+        p36 = small("p36")
+        sum_p36 = small("sum_p36", 1)
+        nc.vector.scalar_tensor_tensor(p36[:], neg_t1[:], -36.0, sum_tb[:], ALU.mult, ALU.mult, accum_out=sum_p36[:])
+        neg_iz = small("neg_iz", 1)
+        nc.vector.reciprocal(neg_iz[:], neg_z[:])
+        w36 = small("w36")
+        nc.vector.scalar_tensor_tensor(w36[:], tanh[:], 1.0, p36[:], ALU.subtract, ALU.mult)
+        neg_rho = small("neg_rho", 1)
+        nc.vector.tensor_tensor(neg_rho[:], sum_p36[:], neg_iz[:], ALU.mult)
+
+        dr = small("dr")
+        nc.vector.tensor_reduce(dr[:], by_page(drr[:]), AXIS_X, ALU.add)
+        j36 = small("j36")
+        nc.vector.scalar_tensor_tensor(j36[:], neg_q0[:, :PAGES], neg_rho[:], p36[:], ALU.mult, ALU.subtract)
+        neg_r = small("neg_r")
+        nc.vector.scalar_tensor_tensor(neg_r[:], dr[:], neg_iz[:], inv_s[:], ALU.mult, ALU.mult)
+        h36 = small("h36")
+        nc.vector.scalar_tensor_tensor(h36[:], neg_t1[:], neg_rho[:], w36[:], ALU.mult, ALU.add)
+
+        terms3 = small("terms3")
+        s3 = small("s3", 1)
+        nc.vector.scalar_tensor_tensor(terms3[:], j36[:], neg_iz[:], neg_r[:], ALU.mult, ALU.mult, accum_out=s3[:])
+        terms1 = small("terms1")
+        neg_s1 = small("neg_s1", 1)
+        nc.vector.scalar_tensor_tensor(
+            terms1[:], neg_q0[:, :PAGES], neg_iz[:], neg_r[:], ALU.mult, ALU.mult, accum_out=neg_s1[:]
+        )
+        part_b = small("part_b", SLOTS)
+        nc.scalar.activation(by_page(part_b[:]), over_page(tanh[:]), ACT.Identity, bias=s3[:], scale=s3[:])
+        part_a = small("part_a", SLOTS)
+        nc.vector.scalar_tensor_tensor(
+            by_page(part_a[:]), over_page(neg_r[:]), neg_s1[:], over_page(h36[:]), ALU.subtract, ALU.mult
+        )
+        nc.vector.tensor_tensor(placed[:].indirect(offsets[:]), part_a[:], part_b[:], ALU.add)
+
+        start = 0
+        for n, width in enumerate(STORE_WIDTHS):
+            cols = slice(start, start + width)
+            result = small("result%d" % n, width)
+            nc.vector.tensor_tensor(result[:], base_sb[:, cols], placed[:, cols], ALU.add)
+            nc.sync.dma_start(out=out[:, cols], in_=result[:])
+            start = start + width

@@ -16,14 +16,19 @@ AXIS_X = mybir.AxisListType.X
 
 P = 128
 PACK = 4
+FEATURES = P * PACK
+QUADRANTS = 4
 POOL = 2048
 SLOTS = 512
 ROWS = 128
 PAGE = 8
 PAGES = SLOTS // PAGE
+PAIRS = PAGE // 2
+MX_ALIGN = 64
+GAIN = 36.0
 STORE_WIDTHS = (256, 512, 512, 512, 256)
 
-FLOPS = 4 * 2 * 512 * ROWS * SLOTS
+FLOPS = 4 * 2 * FEATURES * ROWS * SLOTS
 
 
 def tile_attend_hvpagequotas_s_kernel(
@@ -34,6 +39,12 @@ def tile_attend_hvpagequotas_s_kernel(
         sb = ctx.enter_context(tc.tile_pool(name="sb", bufs=1))
         ps = ctx.enter_context(tc.psum_pool(name="ps", bufs=1))
 
+        def floats(name, width, tag=None):
+            return sb.tile([P, width], F32, name=name, tag=tag or name)
+
+        def mx_tile(name, shape, dtype, tag=None):
+            return sb.tile(shape, dtype, name=name, tag=tag or name, align_bytes=MX_ALIGN)
+
         def by_page(ap):
             return ap.rearrange("p (g j) -> p g j", j=PAGE)
 
@@ -41,171 +52,198 @@ def tile_attend_hvpagequotas_s_kernel(
             return ap.unsqueeze(2).to_broadcast([P, PAGES, PAGE])
 
         offsets = sb.tile([P, SLOTS // 16], U16, name="offsets")
-        key_bytes = sb.tile([P, POOL], U8, name="key_bytes", align_bytes=64)
-        val_bytes = sb.tile([P, POOL], U8, name="val_bytes", align_bytes=64)
-        key_words = sb.tile([P, POOL], U16, name="key_words", align_bytes=64)
-        val_words = sb.tile([P, POOL], U16, name="val_words", align_bytes=64)
-        half = sb.tile([P, 1], F32, name="half")
-        minus_one = sb.tile([P, 1], F32, name="minus_one")
-        abs_tanh = sb.tile([P, PAGES + 1], F32, name="abs_tanh")
-        relu_res = sb.tile([P, PAGES + 1], F32, name="relu_res")
-        placed = sb.tile([P, POOL], F32, name="placed")
-        base_sb = sb.tile([P, POOL], F32, name="base_sb")
+        key_bytes = mx_tile("key_bytes", [P, POOL], U8)
+        val_bytes = mx_tile("val_bytes", [P, POOL], U8)
+        key_words = mx_tile("key_words", [P, POOL], U16)
+        half = floats("half", 1)
+        minus_one = floats("minus_one", 1)
+        abs_tanh = floats("abs_tanh", PAGES + 1, tag="after_ln")
+        placed = floats("placed", POOL)
 
-        def load_bytes(queue, tile, scales):
-            for quad in range(4):
-                queue.dma_start(
+        nc.vector.memset(key_bytes[:].bitcast(I32), 0)
+        nc.vector.memset(half[:], 0.5)
+        zero = floats("zero", 1, tag="after_exp")
+        nc.scalar.activation(minus_one[:], half[:], ACT.Copy, scale=-2.0)
+        nc.vector.memset(val_bytes[:].bitcast(I32), 0)
+        nc.vector.memset(zero[:], 0.0)
+        nc.vector.memset(abs_tanh[:, PAGES : PAGES + 1], 1.0)
+        nc.vector.memset(placed[:].bitcast(I32), 0)
+
+        def load_bytes(tile, scales):
+            for quad in range(QUADRANTS):
+                nc.sync.dma_start(
                     out=tile[32 * quad : 32 * quad + 4, :].bitcast(I32),
                     in_=scales[0, 4 * quad : 4 * quad + 4, :].bitcast(I32),
                 )
 
-        nc.vector.memset(key_bytes[:].bitcast(I32), 0)
-        nc.vector.memset(half[:], 0.5)
-        load_bytes(nc.scalar, key_bytes, keys_scales)
-        nc.scalar.activation(minus_one[:], half[:], ACT.Copy, scale=-2.0)
-        nc.vector.memset(val_bytes[:].bitcast(I32), 0)
-        nc.vector.memset(abs_tanh[:, PAGES : PAGES + 1], 1.0)
-        nc.vector.memset(placed[:], 0.0)
-
-        def load_rows(name, rows):
-            raw = sb.tile([P, PACK, ROWS], F32, name=name, tag=name)
-            nc.sync.dma_start(out=raw[:], in_=rows.rearrange("(p j) w -> p j w", j=PACK))
+        def load_rows(name, rows, tag=None):
+            raw = mx_tile(name, [P, PACK, ROWS], F32, tag)
+            nc.sync.dma_start(out=raw[:], in_=rows.rearrange("(p t) w -> p t w", t=PACK))
             return raw
 
-        nc.sync.dma_start(offsets[:], offs)
         nc.sync.dma_start(out=key_words[:].bitcast(I32), in_=keys_words[0].bitcast(I32))
-        raw_q2 = load_rows("raw_q2", query2)
+        nc.sync.dma_start(offsets[:], offs)
+        load_bytes(key_bytes, keys_scales)
         raw_q = load_rows("raw_q", query)
-        load_bytes(nc.sync, val_bytes, vals_scales)
+        raw_q2 = load_rows("raw_q2", query2)
+        raw_gout = load_rows("raw_gout", gout, tag="gout_shifted_vw")
+        raw_dq2 = load_rows("raw_dq2", dquery2, tag="dq2_tanh")
+        load_bytes(val_bytes, vals_scales)
+        val_words = mx_tile("val_words", [P, POOL], U16)
         nc.sync.dma_start(out=val_words[:].bitcast(I32), in_=vals_words[0].bitcast(I32))
-        raw_dq2 = load_rows("raw_dq2", dquery2)
-        raw_gout = load_rows("raw_gout", gout)
+        relu_res = floats("relu_res", PAGES + 1, tag="after_q0")
         nc.sync.dma_start(out=relu_res[:, PAGES : PAGES + 1], in_=reserve)
+        base_sb = floats("base_sb", POOL)
         nc.sync.dma_start(out=base_sb[:], in_=base)
 
-        def gather(name, window, dtype, tag):
-            picked = sb.tile([P, SLOTS], dtype, name=name, tag=tag, align_bytes=64)
+        def gather(name, window, dtype, tag=None):
+            picked = mx_tile(name, [P, SLOTS], dtype, tag)
             nc.vector.tensor_copy(picked[:], window[:].indirect(offsets[:]))
             return picked
 
         def interleave(name, raws):
-            woven = sb.tile([P, len(raws), ROWS, PACK], BF16, name=name, tag=name, align_bytes=64)
+            woven = mx_tile(name, [P, len(raws), ROWS, PACK], BF16)
             for n, raw in enumerate(raws):
-                nc.scalar.copy(out=woven[:, n], in_=raw[:].rearrange("p j w -> p w j"))
+                nc.scalar.copy(out=woven[:, n], in_=raw[:].rearrange("p t w -> p w t"))
             return woven
 
-        def quantise(name, woven, count):
-            codes = sb.tile([P, count * ROWS], U32, name=name + "_codes", align_bytes=64)
-            scales = sb.tile([P, count * ROWS], U8, name=name + "_scales", align_bytes=64)
+        def quantise(name, woven):
+            width = woven.shape[1] * ROWS
+            codes = mx_tile(name + "_codes", [P, width], U32)
+            scales = mx_tile(name + "_scales", [P, width], U8)
             nc.vector.quantize_mx(
-                out=codes[:].bitcast(FP8X4), scales=scales[:], in_=woven[:].rearrange("p n w j -> p (n w j)")
+                out=codes[:].bitcast(FP8X4), scales=scales[:], in_=woven[:].rearrange("p n w t -> p (n w t)")
             )
             return codes, scales
 
-        def scores(name, rows, n, words, byts):
+        def product(bank, rows, n, words, scale_bytes, start, stop):
             codes, scales = rows
-            bank = ps.tile([ROWS, SLOTS], F32, name=name)
             cols = slice(n * ROWS, (n + 1) * ROWS)
             nc.tensor.matmul_mx(
                 out=bank[:],
                 lhsT=codes[:, cols].bitcast(FP8X4),
                 lhsT_scale=scales[:, cols],
-                rhs=words[:].bitcast(FP4X4),
-                rhs_scale=byts[:],
-                start=True,
-                stop=True,
+                rhs=words.bitcast(FP4X4),
+                rhs_scale=scale_bytes,
+                start=start,
+                stop=stop,
             )
+
+        def scores(name, rows, n, words, scale_bytes):
+            bank = ps.tile([ROWS, SLOTS], F32, name=name)
+            product(bank, rows, n, words[:], scale_bytes[:], True, True)
             return bank
 
-        def small(name, width=PAGES):
-            return sb.tile([P, width], F32, name=name)
+        def deal(dealt, picked, pair_dtype):
+            nc.vector.tensor_copy(
+                dealt.bitcast(pair_dtype).rearrange("p (u g) -> p g u", u=PAIRS),
+                picked[:].bitcast(pair_dtype).rearrange("p (g u) -> p g u", u=PAIRS),
+            )
+            return dealt
 
-        woven_a = interleave("woven_a", [raw_q2, raw_q])
-        woven_b = interleave("woven_b", [raw_dq2, raw_gout])
+        def pair_sums(name, rows, n, words, scale_bytes):
+            bank = ps.tile([ROWS, 2 * PAGES], F32, name=name)
+            for u in range(PAIRS):
+                part = slice(u * 2 * PAGES, (u + 1) * 2 * PAGES)
+                product(bank, rows, n, words[:, part], scale_bytes[:, part], u == 0, u == PAIRS - 1)
+            return bank[:].rearrange("p (g e) -> p g e", e=2)
 
-        kb = gather("kb", key_bytes, U8, "kb")
-        kw = gather("kw", key_words, U16, "kw")
-        first = quantise("first", woven_a, 2)
-        b = scores("b", first, 0, kw, kb)
-        a = scores("a", first, 1, kw, kb)
-        vb = gather("vb", val_bytes, U8, "vb")
+        woven_q_q2 = interleave("woven_q_q2", [raw_q, raw_q2])
+        kw = gather("kw", key_words, U16)
+        woven_gout_dq2 = interleave("woven_gout_dq2", [raw_gout, raw_dq2])
+        kb = gather("kb", key_bytes, U8)
+        mx_q_q2 = quantise("mx_q_q2", woven_q_q2)
+        a = scores("a", mx_q_q2, 0, kw, kb)
+        dealt = mx_tile("dealt", [P, 3 * SLOTS], U8, tag="woven_q_q2")
+        kw_dealt = deal(dealt[:, : 2 * SLOTS].bitcast(U16), kw, I32)
+        kb_dealt = deal(dealt[:, 2 * SLOTS :], kb, U16)
+        b = pair_sums("b", mx_q_q2, 1, kw_dealt, kb_dealt)
 
-        sum_b = small("sum_b")
-        nc.vector.tensor_reduce(sum_b[:], by_page(b[:]), AXIS_X, ALU.add)
-        top = small("top")
+        top = floats("top", PAGES)
         nc.vector.tensor_reduce(top[:], by_page(a[:]), AXIS_X, ALU.max)
-        shifted = small("shifted", SLOTS)
+        shifted = mx_tile("shifted", [P, SLOTS], F32, tag="gout_shifted_vw")
+        sum_b = mx_tile("sum_b", [P, PAGES], F32, tag="sum_b_vb")
+        nc.vector.tensor_reduce(sum_b[:], b, AXIS_X, ALU.add)
         nc.vector.tensor_tensor(by_page(shifted[:]), by_page(a[:]), over_page(top[:]), ALU.subtract)
 
-        tanh = sb.tile([P, PAGES], F32, name="tanh", tag="raw_gout")
+        tanh = mx_tile("tanh", [P, PAGES], F32, tag="dq2_tanh")
         nc.scalar.activation(tanh[:], sum_b[:], ACT.Tanh, scale=3.0 / 16.0)
         nc.scalar.activation(relu_res[:, :PAGES], sum_b[:], ACT.Relu, scale=3.0 / 8.0)
         nc.scalar.activation(abs_tanh[:, :PAGES], tanh[:], ACT.Abs)
-        neg_t1 = small("neg_t1")
+        neg_t1 = floats("neg_t1", PAGES)
         nc.scalar.activation(neg_t1[:], tanh[:], ACT.Identity, bias=minus_one[:], scale=-1.0)
-        pa = sb.tile([P, SLOTS], F32, name="pa", tag="raw_dq2")
-        nc.scalar.activation(pa[:], shifted[:], ACT.Exp)
-        log_sig = shifted[:, : PAGES + 1]
-        nc.scalar.activation(log_sig, abs_tanh[:], ACT.Ln, bias=half[:], scale=0.5)
+        pa = floats("pa", SLOTS)
+        nc.scalar.activation(pa[:], shifted[:], ACT.Exp, bias=zero[:])
+        log_sig = floats("log_sig", PAGES + 1, tag="after_exp")
+        nc.scalar.activation(log_sig[:], abs_tanh[:], ACT.Ln, bias=half[:], scale=0.5)
 
-        second = quantise("second", woven_b, 2)
-        tb = scores("tb", second, 0, kw, kb)
-        vw = gather("vw", val_words, U16, "woven_b")
-        c0 = scores("c0", second, 1, vw, vb)
-
-        s = small("s")
+        mx_gout_dq2 = quantise("mx_gout_dq2", woven_gout_dq2)
+        tb = pair_sums("tb", mx_gout_dq2, 1, kw_dealt, kb_dealt)
+        vb = gather("vb", val_bytes, U8, tag="sum_b_vb")
+        s = floats("s", PAGES)
         nc.vector.tensor_reduce(s[:], by_page(pa[:]), AXIS_X, ALU.add)
-        inv_s = small("inv_s")
-        sum_tb = small("sum_tb")
-        nc.vector.tensor_reduce(sum_tb[:], by_page(tb[:]), AXIS_X, ALU.add)
-        nc.vector.reciprocal(inv_s[:], s[:])
-        drr = small("drr", SLOTS)
-        nc.vector.tensor_tensor(drr[:], c0[:], pa[:], ALU.mult)
+        log_s = floats("log_s", PAGES)
+        nc.scalar.activation(log_s[:], s[:], ACT.Ln)
+        inv_s = floats("inv_s", PAGES)
+        nc.scalar.activation(inv_s[:], log_s[:], ACT.Exp, scale=-1.0)
 
-        neg_q0 = small("neg_q0", PAGES + 1)
-        neg_z = small("neg_z", 1)
+        vw = gather("vw", val_words, U16, tag="gout_shifted_vw")
+        c0 = scores("c0", mx_gout_dq2, 0, vw, vb)
+
+        sum_tb = floats("sum_tb", PAGES, tag="after_ln")
+        nc.vector.tensor_reduce(sum_tb[:], tb, AXIS_X, ALU.add)
+        neg_q0 = floats("neg_q0", PAGES + 1)
+        neg_z = floats("neg_z", 1)
         nc.vector.scalar_tensor_tensor(
-            neg_q0[:], relu_res[:], -1.0, log_sig, ALU.mult, ALU.add, accum_out=neg_z[:]
+            neg_q0[:], relu_res[:], -1.0, log_sig[:], ALU.mult, ALU.add, accum_out=neg_z[:]
         )
-        p36 = small("p36")
-        sum_p36 = small("sum_p36", 1)
-        nc.vector.scalar_tensor_tensor(p36[:], neg_t1[:], -36.0, sum_tb[:], ALU.mult, ALU.mult, accum_out=sum_p36[:])
-        neg_iz = small("neg_iz", 1)
+        u_page = floats("u_page", PAGES)
+        sum_u = floats("sum_u", 1)
+        nc.vector.scalar_tensor_tensor(
+            u_page[:], neg_t1[:], -GAIN, sum_tb[:], ALU.mult, ALU.mult, accum_out=sum_u[:]
+        )
+        neg_iz = floats("neg_iz", 1)
         nc.vector.reciprocal(neg_iz[:], neg_z[:])
-        w36 = small("w36")
-        nc.vector.scalar_tensor_tensor(w36[:], tanh[:], 1.0, p36[:], ALU.subtract, ALU.mult)
-        neg_rho = small("neg_rho", 1)
-        nc.vector.tensor_tensor(neg_rho[:], sum_p36[:], neg_iz[:], ALU.mult)
-
-        dr = small("dr")
+        curved = floats("curved", PAGES)
+        nc.vector.scalar_tensor_tensor(curved[:], tanh[:], 1.0, u_page[:], ALU.subtract, ALU.mult)
+        drr = floats("drr", SLOTS, tag="after_q0")
+        nc.vector.tensor_tensor(drr[:], c0[:], pa[:], ALU.mult)
+        neg_rho = floats("neg_rho", 1)
+        nc.vector.tensor_tensor(neg_rho[:], sum_u[:], neg_iz[:], ALU.mult)
+        dr = floats("dr", PAGES)
         nc.vector.tensor_reduce(dr[:], by_page(drr[:]), AXIS_X, ALU.add)
-        j36 = small("j36")
-        nc.vector.scalar_tensor_tensor(j36[:], neg_q0[:, :PAGES], neg_rho[:], p36[:], ALU.mult, ALU.subtract)
-        neg_r = small("neg_r")
-        nc.vector.scalar_tensor_tensor(neg_r[:], dr[:], neg_iz[:], inv_s[:], ALU.mult, ALU.mult)
-        h36 = small("h36")
-        nc.vector.scalar_tensor_tensor(h36[:], neg_t1[:], neg_rho[:], w36[:], ALU.mult, ALU.add)
+        moved = floats("moved", PAGES)
+        nc.vector.scalar_tensor_tensor(moved[:], neg_q0[:, :PAGES], neg_rho[:], u_page[:], ALU.mult, ALU.subtract)
+        neg_rz = floats("neg_rz", PAGES)
+        nc.vector.scalar_tensor_tensor(neg_rz[:], dr[:], neg_iz[:], inv_s[:], ALU.mult, ALU.mult)
+        slope = floats("slope", PAGES)
+        nc.vector.scalar_tensor_tensor(slope[:], neg_t1[:], neg_rho[:], curved[:], ALU.mult, ALU.add)
 
-        terms3 = small("terms3")
-        s3 = small("s3", 1)
-        nc.vector.scalar_tensor_tensor(terms3[:], j36[:], neg_iz[:], neg_r[:], ALU.mult, ALU.mult, accum_out=s3[:])
-        terms1 = small("terms1")
-        neg_s1 = small("neg_s1", 1)
+        moved_terms = floats("moved_terms", PAGES)
+        moved_sum = floats("moved_sum", 1)
         nc.vector.scalar_tensor_tensor(
-            terms1[:], neg_q0[:, :PAGES], neg_iz[:], neg_r[:], ALU.mult, ALU.mult, accum_out=neg_s1[:]
+            moved_terms[:], moved[:], neg_iz[:], neg_rz[:], ALU.mult, ALU.mult, accum_out=moved_sum[:]
         )
-        part_b = small("part_b", SLOTS)
-        nc.scalar.activation(by_page(part_b[:]), over_page(tanh[:]), ACT.Identity, bias=s3[:], scale=s3[:])
-        part_a = small("part_a", SLOTS)
+        quota_terms = floats("quota_terms", PAGES)
+        neg_quota_sum = floats("neg_quota_sum", 1)
         nc.vector.scalar_tensor_tensor(
-            by_page(part_a[:]), over_page(neg_r[:]), neg_s1[:], over_page(h36[:]), ALU.subtract, ALU.mult
+            quota_terms[:], neg_q0[:, :PAGES], neg_iz[:], neg_rz[:], ALU.mult, ALU.mult, accum_out=neg_quota_sum[:]
         )
-        nc.vector.tensor_tensor(placed[:].indirect(offsets[:]), part_a[:], part_b[:], ALU.add)
+
+        moved_part = floats("moved_part", SLOTS)
+        nc.scalar.activation(
+            by_page(moved_part[:]), over_page(tanh[:]), ACT.Identity, bias=moved_sum[:], scale=moved_sum[:]
+        )
+        slope_part = floats("slope_part", SLOTS)
+        nc.vector.scalar_tensor_tensor(
+            by_page(slope_part[:]), over_page(neg_rz[:]), neg_quota_sum[:], over_page(slope[:]), ALU.subtract, ALU.mult
+        )
+        nc.vector.tensor_tensor(placed[:].indirect(offsets[:]), slope_part[:], moved_part[:], ALU.add)
 
         start = 0
         for n, width in enumerate(STORE_WIDTHS):
             cols = slice(start, start + width)
-            result = small("result%d" % n, width)
+            result = floats("result%d" % n, width)
             nc.vector.tensor_tensor(result[:], base_sb[:, cols], placed[:, cols], ALU.add)
             nc.sync.dma_start(out=out[:, cols], in_=result[:])
             start = start + width

@@ -180,8 +180,15 @@ def tile_attend_hvpagequotas_s_kernel(
         mx_gout_dq2 = quantise("mx_gout_dq2", woven_gout_dq2)
         tb = pair_sums("tb", mx_gout_dq2, 1, kw_dealt, kb_dealt)
         vb = gather("vb", val_bytes, U8, tag="sum_b_vb")
-        s = floats("s", PAGES)
-        nc.vector.tensor_reduce(s[:], by_page(pa[:]), AXIS_X, ALU.add)
+        s = pa
+        per_page = PAGE
+        while per_page > 1:
+            wide = s[:].rearrange("p (g j) -> p g j", j=per_page)
+            per_page = per_page // 2
+            s = floats("s%d" % per_page, PAGES * per_page)
+            nc.gpsimd.tensor_tensor(
+                s[:].rearrange("p (g j) -> p g j", j=per_page), wide[:, :, :per_page], wide[:, :, per_page:], ALU.add
+            )
         log_s = floats("log_s", PAGES)
         nc.scalar.activation(log_s[:], s[:], ACT.Ln)
         inv_s = floats("inv_s", PAGES)

from contextlib import ExitStack

import concourse.mybir as mybir

F32 = mybir.dt.float32
BF16 = mybir.dt.bfloat16
I32 = mybir.dt.int32
U32 = mybir.dt.uint32
U16 = mybir.dt.uint16
U8 = mybir.dt.uint8
FP8X4 = mybir.dt.float8_e4m3fn_x4
FP4X4 = mybir.dt.float4_e2m1fn_x4
ALU = mybir.AluOpType
ACT = mybir.ActivationFunctionType
AXIS_X = mybir.AxisListType.X

P = 128
PACK = 4
FEATURES = P * PACK
QUADRANTS = 4
POOL = 2048
SLOTS = 512
ROWS = 128
PAGE = 8
PAGES = SLOTS // PAGE
PAIRS = PAGE // 2
MX_ALIGN = 64
GAIN = 36.0
STORE_WIDTHS = (256, 512, 512, 512, 256)

FLOPS = 4 * 2 * FEATURES * ROWS * SLOTS


def tile_attend_hvpagequotas_s_kernel(
    tc, query, query2, keys_words, keys_scales, reserve, gout, vals_words, vals_scales, dquery2, base, offs, out
):
    nc = tc.nc
    with ExitStack() as ctx:
        sb = ctx.enter_context(tc.tile_pool(name="sb", bufs=1))
        ps = ctx.enter_context(tc.psum_pool(name="ps", bufs=1))

        def floats(name, width, tag=None):
            return sb.tile([P, width], F32, name=name, tag=tag or name)

        def mx_tile(name, shape, dtype, tag=None):
            return sb.tile(shape, dtype, name=name, tag=tag or name, align_bytes=MX_ALIGN)

        def by_page(ap):
            return ap.rearrange("p (g j) -> p g j", j=PAGE)

        def over_page(ap):
            return ap.unsqueeze(2).to_broadcast([P, PAGES, PAGE])

        offsets = sb.tile([P, SLOTS // 16], U16, name="offsets")
        key_bytes = mx_tile("key_bytes", [P, POOL], U8)
        val_bytes = mx_tile("val_bytes", [P, POOL], U8)
        key_words = mx_tile("key_words", [P, POOL], U16)
        half = floats("half", 1)
        minus_one = floats("minus_one", 1)
        abs_tanh = floats("abs_tanh", PAGES + 1, tag="after_ln")
        placed = floats("placed", POOL)

        nc.vector.memset(key_bytes[:].bitcast(I32), 0)
        nc.vector.memset(half[:], 0.5)
        zero = floats("zero", 1, tag="after_exp")
        nc.scalar.activation(minus_one[:], half[:], ACT.Copy, scale=-2.0)
        nc.vector.memset(val_bytes[:].bitcast(I32), 0)
        nc.vector.memset(zero[:], 0.0)
        nc.vector.memset(abs_tanh[:, PAGES : PAGES + 1], 1.0)
        nc.vector.memset(placed[:].bitcast(I32), 0)

        def load_bytes(tile, scales):
            for quad in range(QUADRANTS):
                nc.sync.dma_start(
                    out=tile[32 * quad : 32 * quad + 4, :].bitcast(I32),
                    in_=scales[0, 4 * quad : 4 * quad + 4, :].bitcast(I32),
                )

        def load_rows(name, rows, tag=None):
            raw = mx_tile(name, [P, PACK, ROWS], F32, tag)
            nc.sync.dma_start(out=raw[:], in_=rows.rearrange("(p t) w -> p t w", t=PACK))
            return raw

        nc.sync.dma_start(out=key_words[:].bitcast(I32), in_=keys_words[0].bitcast(I32))
        nc.sync.dma_start(offsets[:], offs)
        load_bytes(key_bytes, keys_scales)
        raw_q = load_rows("raw_q", query)
        raw_q2 = load_rows("raw_q2", query2)
        raw_gout = load_rows("raw_gout", gout, tag="gout_shifted_vw")
        raw_dq2 = load_rows("raw_dq2", dquery2, tag="dq2_tanh")
        load_bytes(val_bytes, vals_scales)
        val_words = mx_tile("val_words", [P, POOL], U16)
        nc.sync.dma_start(out=val_words[:].bitcast(I32), in_=vals_words[0].bitcast(I32))
        relu_res = floats("relu_res", PAGES + 1, tag="after_q0")
        nc.sync.dma_start(out=relu_res[:, PAGES : PAGES + 1], in_=reserve)
        base_sb = floats("base_sb", POOL)
        nc.sync.dma_start(out=base_sb[:], in_=base)

        def gather(name, window, dtype, tag=None):
            picked = mx_tile(name, [P, SLOTS], dtype, tag)
            nc.vector.tensor_copy(picked[:], window[:].indirect(offsets[:]))
            return picked

        def interleave(name, raws):
            woven = mx_tile(name, [P, len(raws), ROWS, PACK], BF16)
            for n, raw in enumerate(raws):
                nc.scalar.copy(out=woven[:, n], in_=raw[:].rearrange("p t w -> p w t"))
            return woven

        def quantise(name, woven):
            width = woven.shape[1] * ROWS
            codes = mx_tile(name + "_codes", [P, width], U32)
            scales = mx_tile(name + "_scales", [P, width], U8)
            nc.vector.quantize_mx(
                out=codes[:].bitcast(FP8X4), scales=scales[:], in_=woven[:].rearrange("p n w t -> p (n w t)")
            )
            return codes, scales

        def product(bank, rows, n, words, scale_bytes, start, stop):
            codes, scales = rows
            cols = slice(n * ROWS, (n + 1) * ROWS)
            nc.tensor.matmul_mx(
                out=bank[:],
                lhsT=codes[:, cols].bitcast(FP8X4),
                lhsT_scale=scales[:, cols],
                rhs=words.bitcast(FP4X4),
                rhs_scale=scale_bytes,
                start=start,
                stop=stop,
            )

        def scores(name, rows, n, words, scale_bytes):
            bank = ps.tile([ROWS, SLOTS], F32, name=name)
            product(bank, rows, n, words[:], scale_bytes[:], True, True)
            return bank

        def deal(dealt, picked, pair_dtype):
            nc.vector.tensor_copy(
                dealt.bitcast(pair_dtype).rearrange("p (u g) -> p g u", u=PAIRS),
                picked[:].bitcast(pair_dtype).rearrange("p (g u) -> p g u", u=PAIRS),
            )
            return dealt

        def pair_sums(name, rows, n, words, scale_bytes):
            bank = ps.tile([ROWS, 2 * PAGES], F32, name=name)
            for u in range(PAIRS):
                part = slice(u * 2 * PAGES, (u + 1) * 2 * PAGES)
                product(bank, rows, n, words[:, part], scale_bytes[:, part], u == 0, u == PAIRS - 1)
            return bank[:].rearrange("p (g e) -> p g e", e=2)

        woven_q_q2 = interleave("woven_q_q2", [raw_q, raw_q2])
        kw = gather("kw", key_words, U16)
        woven_gout_dq2 = interleave("woven_gout_dq2", [raw_gout, raw_dq2])
        kb = gather("kb", key_bytes, U8)
        mx_q_q2 = quantise("mx_q_q2", woven_q_q2)
        a = scores("a", mx_q_q2, 0, kw, kb)
        dealt = mx_tile("dealt", [P, 3 * SLOTS], U8, tag="woven_q_q2")
        kw_dealt = deal(dealt[:, : 2 * SLOTS].bitcast(U16), kw, I32)
        kb_dealt = deal(dealt[:, 2 * SLOTS :], kb, U16)
        b = pair_sums("b", mx_q_q2, 1, kw_dealt, kb_dealt)

        top = floats("top", PAGES)
        nc.vector.tensor_reduce(top[:], by_page(a[:]), AXIS_X, ALU.max)
        shifted = mx_tile("shifted", [P, SLOTS], F32, tag="gout_shifted_vw")
        sum_b = mx_tile("sum_b", [P, PAGES], F32, tag="sum_b_vb")
        nc.vector.tensor_reduce(sum_b[:], b, AXIS_X, ALU.add)
        nc.vector.tensor_tensor(by_page(shifted[:]), by_page(a[:]), over_page(top[:]), ALU.subtract)

        tanh = mx_tile("tanh", [P, PAGES], F32, tag="dq2_tanh")
        nc.scalar.activation(tanh[:], sum_b[:], ACT.Tanh, scale=3.0 / 16.0)
        nc.scalar.activation(relu_res[:, :PAGES], sum_b[:], ACT.Relu, scale=3.0 / 8.0)
        nc.scalar.activation(abs_tanh[:, :PAGES], tanh[:], ACT.Abs)
        neg_t1 = floats("neg_t1", PAGES)
        nc.scalar.activation(neg_t1[:], tanh[:], ACT.Identity, bias=minus_one[:], scale=-1.0)
        pa = floats("pa", SLOTS)
        nc.scalar.activation(pa[:], shifted[:], ACT.Exp, bias=zero[:])
        log_sig = floats("log_sig", PAGES + 1, tag="after_exp")
        nc.scalar.activation(log_sig[:], abs_tanh[:], ACT.Ln, bias=half[:], scale=0.5)

        mx_gout_dq2 = quantise("mx_gout_dq2", woven_gout_dq2)
        tb = pair_sums("tb", mx_gout_dq2, 1, kw_dealt, kb_dealt)
        vb = gather("vb", val_bytes, U8, tag="sum_b_vb")
        s = pa
        per_page = PAGE
        while per_page > 1:
            wide = s[:].rearrange("p (g j) -> p g j", j=per_page)
            per_page = per_page // 2
            s = floats("s%d" % per_page, PAGES * per_page)
            nc.gpsimd.tensor_tensor(
                s[:].rearrange("p (g j) -> p g j", j=per_page), wide[:, :, :per_page], wide[:, :, per_page:], ALU.add
            )
        log_s = floats("log_s", PAGES)
        nc.scalar.activation(log_s[:], s[:], ACT.Ln)
        inv_s = floats("inv_s", PAGES)
        nc.scalar.activation(inv_s[:], log_s[:], ACT.Exp, scale=-1.0)

        vw = gather("vw", val_words, U16, tag="gout_shifted_vw")
        c0 = scores("c0", mx_gout_dq2, 0, vw, vb)

        sum_tb = floats("sum_tb", PAGES, tag="after_ln")
        nc.vector.tensor_reduce(sum_tb[:], tb, AXIS_X, ALU.add)
        neg_q0 = floats("neg_q0", PAGES + 1)
        neg_z = floats("neg_z", 1)
        nc.vector.scalar_tensor_tensor(
            neg_q0[:], relu_res[:], -1.0, log_sig[:], ALU.mult, ALU.add, accum_out=neg_z[:]
        )
        u_page = floats("u_page", PAGES)
        sum_u = floats("sum_u", 1)
        nc.vector.scalar_tensor_tensor(
            u_page[:], neg_t1[:], -GAIN, sum_tb[:], ALU.mult, ALU.mult, accum_out=sum_u[:]
        )
        neg_iz = floats("neg_iz", 1)
        nc.vector.reciprocal(neg_iz[:], neg_z[:])
        curved = floats("curved", PAGES)
        nc.vector.scalar_tensor_tensor(curved[:], tanh[:], 1.0, u_page[:], ALU.subtract, ALU.mult)
        drr = floats("drr", SLOTS, tag="after_q0")
        nc.vector.tensor_tensor(drr[:], c0[:], pa[:], ALU.mult)
        neg_rho = floats("neg_rho", 1)
        nc.vector.tensor_tensor(neg_rho[:], sum_u[:], neg_iz[:], ALU.mult)
        dr = floats("dr", PAGES)
        nc.vector.tensor_reduce(dr[:], by_page(drr[:]), AXIS_X, ALU.add)
        moved = floats("moved", PAGES)
        nc.vector.scalar_tensor_tensor(moved[:], neg_q0[:, :PAGES], neg_rho[:], u_page[:], ALU.mult, ALU.subtract)
        neg_rz = floats("neg_rz", PAGES)
        nc.vector.scalar_tensor_tensor(neg_rz[:], dr[:], neg_iz[:], inv_s[:], ALU.mult, ALU.mult)
        slope = floats("slope", PAGES)
        nc.vector.scalar_tensor_tensor(slope[:], neg_t1[:], neg_rho[:], curved[:], ALU.mult, ALU.add)

        moved_terms = floats("moved_terms", PAGES)
        moved_sum = floats("moved_sum", 1)
        nc.vector.scalar_tensor_tensor(
            moved_terms[:], moved[:], neg_iz[:], neg_rz[:], ALU.mult, ALU.mult, accum_out=moved_sum[:]
        )
        quota_terms = floats("quota_terms", PAGES)
        neg_quota_sum = floats("neg_quota_sum", 1)
        nc.vector.scalar_tensor_tensor(
            quota_terms[:], neg_q0[:, :PAGES], neg_iz[:], neg_rz[:], ALU.mult, ALU.mult, accum_out=neg_quota_sum[:]
        )

        moved_part = floats("moved_part", SLOTS)
        nc.scalar.activation(
            by_page(moved_part[:]), over_page(tanh[:]), ACT.Identity, bias=moved_sum[:], scale=moved_sum[:]
        )
        slope_part = floats("slope_part", SLOTS)
        nc.vector.scalar_tensor_tensor(
            by_page(slope_part[:]), over_page(neg_rz[:]), neg_quota_sum[:], over_page(slope[:]), ALU.subtract, ALU.mult
        )
        nc.vector.tensor_tensor(placed[:].indirect(offsets[:]), slope_part[:], moved_part[:], ALU.add)

        start = 0
        for n, width in enumerate(STORE_WIDTHS):
            cols = slice(start, start + width)
            result = floats("result%d" % n, width)
            nc.vector.tensor_tensor(result[:], base_sb[:, cols], placed[:, cols], ALU.add)
            nc.sync.dma_start(out=out[:, cols], in_=result[:])
            start = start + width
